import numpy as np
import ml_dtypes


def mxq(x, axis, fmt="e4m3"):
    dtype, down = {"e4m3": (ml_dtypes.float8_e4m3fn, 7), "e5m2": (ml_dtypes.float8_e5m2, 14)}[fmt]
    v = np.moveaxis(np.asarray(x, np.float32).astype(ml_dtypes.bfloat16).astype(np.float64), axis, -1)
    blocks = v.reshape(v.shape[:-1] + (-1, 32))
    amax = np.abs(blocks).max(-1, keepdims=True)
    byte = np.maximum(np.where(amax > 0, np.frexp(amax)[1] - 1 + 127, 0) - down, 1)
    scale = np.exp2(byte - 127.0)
    codes = (blocks / scale).astype(np.float32).astype(dtype).astype(np.float64)
    return np.moveaxis((codes * scale).reshape(v.shape), -1, axis)


WIDE = False


def mx_kscale(k):
    if not WIDE:
        return np.ones(k)
    levels = np.array([10, -10, 5, -5, 0])
    if k % 512:
        return np.exp2(np.random.permutation(np.resize(levels, k // 32))).repeat(32)
    a = np.empty((k // 512, 16))
    for p in range(k // 512):
        a[p, :8] = np.random.permutation(np.resize(levels, 8))
        for g in range(8):
            far = levels[np.abs(levels - a[p, g]) >= 10]
            a[p, g + 8] = far[np.random.randint(len(far))]
    return np.exp2(a.ravel()).repeat(32)


BF16 = ml_dtypes.bfloat16


def bf(x):
    return np.asarray(x, np.float32).astype(BF16)


def f64(x):
    return np.asarray(x).astype(np.float64)

def planes(Y):
    n, m = Y.shape
    b = f64(bf(Y)).reshape(n // 32, 32, m)
    amax = np.abs(b).max(1)
    byte = np.clip(np.where(amax > 0, np.frexp(amax)[1] - 1 + 127 - 7, 1), 1, 254)
    codes = (b * np.exp2(127.0 - byte)[:, None, :]).reshape(n, m).astype(np.float32).astype(ml_dtypes.float8_e4m3fn).view(np.uint8)
    words = codes.reshape(n // 512, 128, 4, m).transpose(0, 1, 3, 2)
    return np.ascontiguousarray(words), np.ascontiguousarray(byte.astype(np.uint8).reshape(n // 512, 16, m))


B, M, N = 2, 512, 1024


def row_norm(x):
    return np.sqrt(np.sum(x * x, axis=-1, keepdims=True))


def setup_inputs():
    s, t = mx_kscale(M), mx_kscale(N)
    dl = np.random.uniform(0.5, 2.0, (B, M, 1))
    dm = np.random.uniform(0.5, 2.0, (B, M, 1))
    return {
        "l": bf(np.random.standard_normal((B, M, M)) / np.sqrt(M) * dl * s[None, None, :]),
        "g": bf(np.random.standard_normal((B, M, N)) / s[None, :, None] * t[None, None, :]),
        "r": bf(np.random.standard_normal((B, N, N)) / np.sqrt(N) / t[None, :, None]),
        "m": bf(np.random.standard_normal((B, M, N)) * 0.7 * dm),
        "v": bf(np.random.uniform(0.2, 1.5, (B, M, N))),
    }


def core(l, g, r, m, v):
    h = mxq(f64(l), 2, "e4m3") @ mxq(f64(g), 1, "e4m3")
    p = mxq(h, 2, "e4m3") @ mxq(f64(r), 1, "e4m3")

    a = f64(m) / (np.sqrt(f64(v)) + 0.1)

    norm_a = row_norm(a)
    norm_p = row_norm(p)

    return 0.7 * p * (norm_a / (norm_p + 1e-6)) + 0.3 * a


def reference(l, g, r, m, v):
    R_out = core(l, g, r, m, v)
    words, scales = planes(np.moveaxis(R_out, 2, 0).reshape(1024, -1))
    return R_out, words, scales

@@ -1,0 +1,428 @@
+from contextlib import ExitStack
+
+import concourse.mybir as mybir
+from concourse.masks import make_identity
+
+F32 = mybir.dt.float32
+BF16 = mybir.dt.bfloat16
+U32 = mybir.dt.uint32
+I32 = mybir.dt.int32
+U8 = mybir.dt.uint8
+X4 = mybir.dt.float8_e4m3fn_x4
+ACT = mybir.ActivationFunctionType
+ALU = mybir.AluOpType
+
+B, M, N = 2, 512, 1024
+FLOPS = 2 * B * (M * M * N + M * N * N)
+P = 128
+PACK = 4
+KP = P * PACK
+G = N // KP
+H = N // 512
+RT = M // P
+T = B * RT
+
+
+def tile_blockshampooadamgraftstep_x1_kernel(tc, l, g, r, m, v, out_0, out_1, out_2):
+    nc = tc.nc
+    with ExitStack() as ctx:
+        keep = ctx.enter_context(tc.tile_pool(name="keep", bufs=1))
+        work = ctx.enter_context(tc.tile_pool(name="work", bufs=3))
+        psum = ctx.enter_context(tc.psum_pool(name="psum", bufs=6))
+        psum_t = ctx.enter_context(tc.psum_pool(name="psum_t", bufs=2))
+
+        ident = keep.tile([P, P], F32, name="ident")
+        half = keep.tile([P, 2], F32, name="half")
+        minus1 = keep.tile([P, 1], F32, name="minus1")
+        junk = keep.tile([P, N], BF16, name="junk")
+
+        def keep_tiles(name, count, shape, dtype):
+            return [keep.tile(shape, dtype, name=name + str(i), align_bytes=64) for i in range(count)]
+
+        v_raw = keep_tiles("v_raw", T, [P, N], BF16)
+        m_raw = keep_tiles("m_raw", T, [P, N], BF16)
+        u = keep_tiles("u", T, [P, N], F32)
+        l_raw = keep_tiles("l_raw", B, [P, RT, M], BF16)
+        l_il = keep_tiles("l_il", B, [P, M * PACK], BF16)
+        l_codes = keep_tiles("l_codes", B, [P, M], U32)
+        l_scales = keep_tiles("l_scales", B, [P, M], U8)
+        g_codes = keep_tiles("g_codes", B * G, [P, KP], U32)
+        g_scales = keep_tiles("g_scales", B * G, [P, KP], U8)
+        r_codes = keep_tiles("r_codes", B * G, [P, N], U32)
+        r_scales = keep_tiles("r_scales", B * G, [P, N], U8)
+        h_codes = keep_tiles("h_codes", T, [P, G * P], U32)
+        h_scales = keep_tiles("h_scales", T, [P, G * P], U8)
+        o_codes = keep_tiles("o_codes", T, [P, G, P], U32)
+        o_scales = keep_tiles("o_scales", B, [P, G, M], U8)
+        sums = keep_tiles("sums", T, [P, 2], F32)
+        squares = keep_tiles("squares", T, [P, 2], F32)
+        roots = keep_tiles("roots", T, [P, 2], F32)
+        dens = keep_tiles("dens", T, [P, 1], F32)
+        invs = keep_tiles("invs", T, [P, 1], F32)
+        factors = keep_tiles("factors", T, [P, 1], F32)
+
+        words_out = out_1.bitcast(I32).rearrange("g p m o -> p g (m o)")
+        scales_out = out_2.bitcast(I32)
+
+        def rows(t):
+            return t // RT, slice((t % RT) * P, (t % RT + 1) * P)
+
+        def load_v(t):
+            b, rs = rows(t)
+            nc.sync.dma_start(out=v_raw[t][:], in_=v[b, rs, :])
+
+        def load_m(t):
+            b, rs = rows(t)
+            nc.sync.dma_start(out=m_raw[t][:], in_=m[b, rs, :])
+
+        def load_l(b):
+            nc.sync.dma_start(out=l_raw[b][:], in_=l[b].rearrange("(i p) k -> p i k", p=P))
+
+        g_raw = {}
+        r_raw = {}
+
+        def load_g(b, q):
+            t = work.tile([P, PACK, KP], BF16, name="g_raw", bufs=4, align_bytes=64)
+            g_raw[b, q] = t
+            nc.sync.dma_start(out=t[:], in_=g[b, :, q * KP:(q + 1) * KP].rearrange("(p j) n -> p j n", j=PACK))
+
+        def load_r(b, q):
+            t = work.tile([P, PACK, N], BF16, name="r_raw", bufs=3, align_bytes=64)
+            r_raw[b, q] = t
+            nc.sync.dma_start(out=t[:], in_=r[b, q * KP:(q + 1) * KP, :].rearrange("(p j) n -> p j n", j=PACK))
+
+        g_il = {}
+        r_il = {}
+
+        def gi(b, q):
+            t = work.tile([P, KP * PACK], BF16, name="g_il", bufs=2, align_bytes=64)
+            g_il[b, q] = t
+            nc.vector.tensor_copy(
+                out=t[:].rearrange("p (t m j) -> p t m j", t=PACK, j=PACK),
+                in_=g_raw[b, q][:].rearrange("p j (m t) -> p t m j", t=PACK))
+
+        def gq(b, q):
+            i = b * G + q
+            nc.vector.quantize_mx(out=g_codes[i][:].bitcast(X4), scales=g_scales[i][:], in_=g_il[b, q][:])
+
+        def ri(b, q, h):
+            t = work.tile([P, 512 * PACK], BF16, name="r_il", bufs=3, align_bytes=64)
+            r_il[b, q, h] = t
+            nc.vector.tensor_copy(
+                out=t[:].rearrange("p (c i j) -> p c j i", i=4, j=PACK),
+                in_=r_raw[b, q][:, :, h * 512:(h + 1) * 512].rearrange("p j (c i) -> p c j i", i=4))
+
+        def rq(b, q, h):
+            i = b * G + q
+            cols = slice(h * 512, (h + 1) * 512)
+            nc.vector.quantize_mx(out=r_codes[i][:, cols].bitcast(X4), scales=r_scales[i][:, cols], in_=r_il[b, q, h][:])
+
+        tr_bank = {}
+
+        def l_turn(b, s):
+            bank = psum_t.tile([P, 2, 2, P], F32, name="tr")
+            tr_bank["l", b, s] = bank
+            for i in range(2):
+                words = l_raw[b][:, 2 * s + i, :].bitcast(F32)
+                for w in range(2):
+                    nc.tensor.transpose(out=bank[:, i, w, :], in_=words[:, w::2], identity=ident[:])
+
+        def copy_on(eng, out, in_):
+            if eng == "V":
+                nc.vector.tensor_copy(out=out, in_=in_)
+            else:
+                nc.scalar.copy(out=out, in_=in_)
+
+        def le(eng, b, s):
+            copy_on(eng, l_il[b][:].bitcast(F32)[:, s * 512:(s + 1) * 512].rearrange("p (i r w) -> p i r w", i=2, w=2),
+                    tr_bank["l", b, s][:].rearrange("p i w r -> p i r w"))
+
+        def lq(b):
+            nc.vector.quantize_mx(out=l_codes[b][:].bitcast(X4), scales=l_scales[b][:], in_=l_il[b][:])
+
+        h_bank = {}
+        h_il = {}
+
+        def h_mm(t, q):
+            b, i = t // RT, b_g(t, q)
+            bank = psum.tile([P, PACK, P], F32, name="bank")
+            h_bank[t, q] = bank
+            cols = rows(t)[1]
+            for k in range(PACK):
+                sc = slice(k * P, (k + 1) * P)
+                nc.tensor.matmul_mx(out=bank[:, k, :], lhsT=g_codes[i][:, sc].bitcast(X4), lhsT_scale=g_scales[i][:, sc],
+                                    rhs=l_codes[b][:, cols].bitcast(X4), rhs_scale=l_scales[b][:, cols], start=True, stop=True)
+
+        def b_g(t, q):
+            return (t // RT) * G + q
+
+        def he(eng, t, q):
+            if q == 0:
+                tile = work.tile([P, G, P, PACK], BF16, name="h_il", bufs=3, align_bytes=64)
+                h_il[t] = tile
+            copy_on(eng, h_il[t][:, q, :, :], h_bank[t, q][:].rearrange("p t i -> p i t"))
+
+        def hq(t):
+            nc.vector.quantize_mx(out=h_codes[t][:].bitcast(X4), scales=h_scales[t][:],
+                                  in_=h_il[t][:].rearrange("p q i t -> p (q i t)"))
+
+        p_bank = {}
+
+        def p_mm(t, h):
+            bank = psum.tile([P, 512], F32, name="bank")
+            p_bank[t, h] = bank
+            cols = slice(h * 512, (h + 1) * 512)
+            for q in range(G):
+                hs = slice(q * P, (q + 1) * P)
+                i = b_g(t, q)
+                nc.tensor.matmul_mx(out=bank[:], lhsT=h_codes[t][:, hs].bitcast(X4), lhsT_scale=h_scales[t][:, hs],
+                                    rhs=r_codes[i][:, cols].bitcast(X4), rhs_scale=r_scales[i][:, cols],
+                                    start=(q == 0), stop=(q == G - 1))
+
+        def ln(t):
+            nc.scalar.activation(out=u[t][:], in_=v_raw[t][:], func=ACT.Ln, scale=100.0)
+
+        def sig(t):
+            nc.scalar.activation(out=u[t][:], in_=u[t][:], func=ACT.Sigmoid, scale=-0.5)
+
+        def ml(t):
+            nc.vector.scalar_tensor_tensor(out=u[t][:], in0=u[t][:], scalar=3.0, in1=m_raw[t][:], op0=ALU.mult, op1=ALU.mult)
+
+        def asq(t):
+            nc.scalar.activation(out=junk[:], in_=u[t][:], func=ACT.Square, accum_out=squares[t][:, 1:2])
+
+        def psq(t, h):
+            nc.scalar.activation(out=junk[:, h * 512:(h + 1) * 512], in_=p_bank[t, h][:], func=ACT.Square,
+                                 accum_out=sums[t][:, h:h + 1])
+
+        def stat(t):
+            nc.gpsimd.tensor_tensor(out=squares[t][:, 0:1], in0=sums[t][:, 0:1], in1=sums[t][:, 1:2], op=ALU.add)
+            nc.gpsimd.tensor_tensor(out=roots[t][:], in0=squares[t][:], in1=half[:], op=ALU.pow)
+            nc.gpsimd.tensor_scalar(out=dens[t][:], in0=roots[t][:, 0:1], scalar1=1.0, scalar2=1e-6, op0=ALU.mult, op1=ALU.add)
+            nc.gpsimd.tensor_tensor(out=invs[t][:], in0=dens[t][:], in1=minus1[:], op=ALU.pow)
+            nc.gpsimd.tensor_scalar(out=factors[t][:], in0=invs[t][:], scalar1=roots[t][:, 1:2], scalar2=7.0 / 3.0,
+                                    op0=ALU.mult, op1=ALU.mult)
+
+        o32 = {}
+        o16 = {}
+        o_il = {}
+
+        def fin(t, h):
+            if h == 0:
+                tile = work.tile([P, N], F32, name="o32", bufs=3)
+                o32[t] = tile
+            cols = slice(h * 512, (h + 1) * 512)
+            nc.vector.scalar_tensor_tensor(out=o32[t][:, cols], in0=p_bank[t, h][:], scalar=factors[t][:, 0:1],
+                                           in1=u[t][:, cols], op0=ALU.mult, op1=ALU.add)
+
+        def store(t):
+            b, rs = rows(t)
+            nc.sync.dma_start(out=out_0[b, rs, :], in_=o32[t][:])
+
+        def cast(t, h):
+            if h == 0:
+                tile = work.tile([P, N], BF16, name="o16", bufs=3)
+                o16[t] = tile
+            cols = slice(h * 512, (h + 1) * 512)
+            nc.vector.tensor_copy(out=o16[t][:, cols], in_=o32[t][:, cols])
+
+        def o_turn(t, q):
+            if q == 0:
+                bank = psum_t.tile([P, G, 2, P], F32, name="tr")
+                tr_bank["o", t] = bank
+            words = o16[t][:].bitcast(F32)
+            for w in range(2):
+                nc.tensor.transpose(out=tr_bank["o", t][:, q, w, :], in_=words[:, q * 256 + w:(q + 1) * 256:2], identity=ident[:])
+
+        def oe_tile(t):
+            tile = work.tile([P, G * P * PACK], BF16, name="o_il", bufs=3, align_bytes=64)
+            o_il[t] = tile
+
+        def oe(eng, t):
+            oe_tile(t)
+            copy_on(eng, o_il[t][:].bitcast(F32).rearrange("p (q r w) -> p q r w", q=G, w=2),
+                    tr_bank["o", t][:].rearrange("p q w r -> p q r w"))
+
+        def oe_half(eng, t, q):
+            if q == 0:
+                oe_tile(t)
+            copy_on(eng, o_il[t][:].bitcast(F32)[:, q * 256:(q + 1) * 256].rearrange("p (r w) -> p r w", w=2),
+                    tr_bank["o", t][:, q, :, :].rearrange("p w r -> p r w"))
+
+        def oq(t, q):
+            b, rs = rows(t)
+            nc.vector.quantize_mx(out=o_codes[t][:, q, :].bitcast(X4), scales=o_scales[b][:, q, rs],
+                                  in_=o_il[t][:, q * 512:(q + 1) * 512])
+
+        def store_words(t):
+            nc.sync.dma_start(out=words_out[:, :, t * P:(t + 1) * P], in_=o_codes[t][:].bitcast(I32))
+
+        def store_scales(b):
+            for q in range(4):
+                nc.sync.dma_start(
+                    out=scales_out[:, 4 * q:4 * q + 4, b * P:(b + 1) * P].rearrange("g r m -> r g m"),
+                    in_=o_scales[b][32 * q:32 * q + 4, :, :].bitcast(I32))
+
+        with tc.manual_schedule():
+            make_identity(nc, ident[:])
+            nc.gpsimd.memset(half[:], 0.5)
+            nc.gpsimd.memset(minus1[:], -1.0)
+            load_g(0, 0)
+            load_v(0)
+            load_v(1)
+            load_l(0)
+            load_g(0, 1)
+            load_v(2)
+            load_v(3)
+            load_r(0, 0)
+            load_v(4)
+            load_v(5)
+            load_r(0, 1)
+            load_v(6)
+            load_v(7)
+            load_g(1, 0)
+            load_l(1)
+            load_g(1, 1)
+            load_r(1, 0)
+            load_m(0)
+            load_m(1)
+
+            ln(0)
+            gi(0, 0)
+            l_turn(0, 0)
+            l_turn(0, 1)
+            ln(1)
+            gq(0, 0)
+            le("S", 0, 0)
+            le("S", 0, 1)
+            gi(0, 1)
+            lq(0)
+            gq(0, 1)
+            for t in range(RT - 1):
+                h_mm(t, 0)
+                h_mm(t, 1)
+            ln(2)
+            ln(3)
+            ln(4)
+            ri(0, 0, 0)
+            ri(0, 0, 1)
+            rq(0, 0, 0)
+            rq(0, 0, 1)
+            for t in range(RT):
+                if t == 1:
+                    h_mm(RT - 1, 0)
+                    h_mm(RT - 1, 1)
+                he("S", t, 0)
+                he("S", t, 1)
+                if t == 0:
+                    load_r(1, 1)
+                    for k in range(2, T):
+                        load_m(k)
+                if t < 3:
+                    ln(5 + t)
+                if t == 0:
+                    ri(0, 1, 0)
+                if t == 1:
+                    ri(0, 1, 1)
+                    hq(0)
+                if t == 2:
+                    rq(0, 1, 0)
+                    hq(1)
+            rq(0, 1, 1)
+            l_turn(1, 0)
+            l_turn(1, 1)
+            gi(1, 0)
+            hq(2)
+            le("S", 1, 0)
+            le("S", 1, 1)
+            gq(1, 0)
+            gi(1, 1)
+            hq(3)
+            lq(1)
+            gq(1, 1)
+            sig(0)
+            sig(1)
+            sig(2)
+            h_mm(4, 0)
+            h_mm(4, 1)
+            he("S", 4, 0)
+            he("S", 4, 1)
+            ri(1, 0, 0)
+            ri(1, 0, 1)
+            ml(0)
+            h_mm(5, 0)
+            h_mm(5, 1)
+            he("S", 5, 0)
+            he("S", 5, 1)
+            rq(1, 0, 0)
+            rq(1, 0, 1)
+            hq(4)
+            h_mm(6, 0)
+            h_mm(6, 1)
+            he("S", 6, 0)
+            he("S", 6, 1)
+            sig(3)
+            ml(1)
+            hq(5)
+            ml(2)
+            hq(6)
+            h_mm(7, 0)
+            h_mm(7, 1)
+
+            def p_of(t):
+                if t < T:
+                    p_mm(t, 0)
+                    p_mm(t, 1)
+
+            def sums_of(t):
+                if t < T:
+                    psq(t, 0)
+                    psq(t, 1)
+                    stat(t)
+            p_of(0)
+            asq(0)
+            sums_of(0)
+            ri(1, 1, 0)
+            ri(1, 1, 1)
+            p_of(1)
+            asq(1)
+            sums_of(1)
+            he("S", 7, 0)
+            he("S", 7, 1)
+            asq(2)
+            ml(3)
+            for t in range(T):
+                p_of(t + 2)
+                fin(t, 0)
+                fin(t, 1)
+                store(t)
+                if t == 0:
+                    rq(1, 1, 0)
+                    rq(1, 1, 1)
+                    hq(7)
+                if t >= 1:
+                    oe_half("S", t - 1, 0)
+                    oe_half("V", t - 1, 1)
+                cast(t, 0)
+                cast(t, 1)
+                o_turn(t, 0)
+                o_turn(t, 1)
+                if t + 4 < T:
+                    sig(t + 4)
+                if t + 3 < T:
+                    asq(t + 3)
+                sums_of(t + 2)
+                if t >= 1:
+                    oq(t - 1, 0)
+                    oq(t - 1, 1)
+                    store_words(t - 1)
+                if t == RT:
+                    store_scales(0)
+                if t + 4 < T:
+                    ml(t + 4)
+            oe_half("S", T - 1, 0)
+            oe_half("V", T - 1, 1)
+            oq(T - 1, 0)
+            oq(T - 1, 1)
+            store_words(T - 1)
+            store_scales(1)

@@ -32,8 +32,6 @@ def tile_blockshampooadamgraftstep_x1_kernel(tc, l, g, r, m, v, out_0, out_1, ou
         psum_t = ctx.enter_context(tc.psum_pool(name="psum_t", bufs=2))
 
         ident = keep.tile([P, P], F32, name="ident")
-        half = keep.tile([P, 2], F32, name="half")
-        minus1 = keep.tile([P, 1], F32, name="minus1")
         junk = keep.tile([P, N], BF16, name="junk")
 
         def keep_tiles(name, count, shape, dtype):
@@ -54,12 +52,13 @@ def tile_blockshampooadamgraftstep_x1_kernel(tc, l, g, r, m, v, out_0, out_1, ou
         h_scales = keep_tiles("h_scales", T, [P, G * P], U8)
         o_codes = keep_tiles("o_codes", T, [P, G, P], U32)
         o_scales = keep_tiles("o_scales", B, [P, G, M], U8)
-        sums = keep_tiles("sums", T, [P, 2], F32)
-        squares = keep_tiles("squares", T, [P, 2], F32)
-        roots = keep_tiles("roots", T, [P, 2], F32)
-        dens = keep_tiles("dens", T, [P, 1], F32)
-        invs = keep_tiles("invs", T, [P, 1], F32)
-        factors = keep_tiles("factors", T, [P, 1], F32)
+        p_sums = keep.tile([P, 2 * T], F32, name="p_sums")
+        a_sums = keep.tile([P, T], F32, name="a_sums")
+        p_norms = keep.tile([P, T], F32, name="p_norms")
+        a_norms = keep.tile([P, T], F32, name="a_norms")
+        dens = keep.tile([P, T], F32, name="dens")
+        invs = keep.tile([P, T], F32, name="invs")
+        factors = keep.tile([P, T], F32, name="factors")
 
         words_out = out_1.bitcast(I32).rearrange("g p m o -> p g (m o)")
         scales_out = out_2.bitcast(I32)
@@ -189,19 +188,28 @@ def tile_blockshampooadamgraftstep_x1_kernel(tc, l, g, r, m, v, out_0, out_1, ou
             nc.vector.scalar_tensor_tensor(out=u[t][:], in0=u[t][:], scalar=3.0, in1=m_raw[t][:], op0=ALU.mult, op1=ALU.mult)
 
         def asq(t):
-            nc.scalar.activation(out=junk[:], in_=u[t][:], func=ACT.Square, accum_out=squares[t][:, 1:2])
+            nc.scalar.activation(out=junk[:], in_=u[t][:], func=ACT.Square, accum_out=a_sums[:, t:t + 1])
 
         def psq(t, h):
             nc.scalar.activation(out=junk[:, h * 512:(h + 1) * 512], in_=p_bank[t, h][:], func=ACT.Square,
-                                 accum_out=sums[t][:, h:h + 1])
+                                 accum_out=p_sums[:, 2 * t + h:2 * t + h + 1])
 
-        def stat(t):
-            nc.gpsimd.tensor_tensor(out=squares[t][:, 0:1], in0=sums[t][:, 0:1], in1=sums[t][:, 1:2], op=ALU.add)
-            nc.gpsimd.tensor_tensor(out=roots[t][:], in0=squares[t][:], in1=half[:], op=ALU.pow)
-            nc.gpsimd.tensor_scalar(out=dens[t][:], in0=roots[t][:, 0:1], scalar1=1.0, scalar2=1e-6, op0=ALU.mult, op1=ALU.add)
-            nc.gpsimd.tensor_tensor(out=invs[t][:], in0=dens[t][:], in1=minus1[:], op=ALU.pow)
-            nc.gpsimd.tensor_scalar(out=factors[t][:], in0=invs[t][:], scalar1=roots[t][:, 1:2], scalar2=7.0 / 3.0,
-                                    op0=ALU.mult, op1=ALU.mult)
+        def a_root(t):
+            nc.scalar.activation(out=a_norms[:, t:t + 2], in_=a_sums[:, t:t + 2], func=ACT.Sqrt, scale=49.0 / 9.0)
+
+        def p_root(t):
+            nc.scalar.activation(out=p_norms[:, t:t + 1], in_=p_sums[:, 2 * t:2 * t + 1], func=ACT.Sqrt,
+                                 bias=p_sums[:, 2 * t + 1:2 * t + 2])
+
+        def den(t):
+            nc.vector.tensor_scalar(out=dens[:, t:t + 1], in0=p_norms[:, t:t + 1], scalar1=1e-6, scalar2=None, op0=ALU.add)
+
+        def inv(t):
+            nc.vector.reciprocal(out=invs[:, t:t + 1], in_=dens[:, t:t + 1])
+
+        def fac(t):
+            nc.vector.tensor_scalar(out=factors[:, t:t + 1], in0=invs[:, t:t + 1], scalar1=a_norms[:, t:t + 1], scalar2=None,
+                                    op0=ALU.mult)
 
         o32 = {}
         o16 = {}
@@ -212,7 +220,7 @@ def tile_blockshampooadamgraftstep_x1_kernel(tc, l, g, r, m, v, out_0, out_1, ou
                 tile = work.tile([P, N], F32, name="o32", bufs=3)
                 o32[t] = tile
             cols = slice(h * 512, (h + 1) * 512)
-            nc.vector.scalar_tensor_tensor(out=o32[t][:, cols], in0=p_bank[t, h][:], scalar=factors[t][:, 0:1],
+            nc.vector.scalar_tensor_tensor(out=o32[t][:, cols], in0=p_bank[t, h][:], scalar=factors[:, t:t + 1],
                                            in1=u[t][:, cols], op0=ALU.mult, op1=ALU.add)
 
         def store(t):
@@ -265,8 +273,6 @@ def tile_blockshampooadamgraftstep_x1_kernel(tc, l, g, r, m, v, out_0, out_1, ou
 
         with tc.manual_schedule():
             make_identity(nc, ident[:])
-            nc.gpsimd.memset(half[:], 0.5)
-            nc.gpsimd.memset(minus1[:], -1.0)
             load_g(0, 0)
             load_v(0)
             load_v(1)
@@ -340,34 +346,34 @@ def tile_blockshampooadamgraftstep_x1_kernel(tc, l, g, r, m, v, out_0, out_1, ou
             hq(3)
             lq(1)
             gq(1, 1)
-            sig(0)
-            sig(1)
-            sig(2)
+            for t in range(T):
+                sig(t)
             h_mm(4, 0)
             h_mm(4, 1)
-            he("S", 4, 0)
-            he("S", 4, 1)
-            ri(1, 0, 0)
-            ri(1, 0, 1)
-            ml(0)
             h_mm(5, 0)
             h_mm(5, 1)
-            he("S", 5, 0)
-            he("S", 5, 1)
+            ri(1, 0, 0)
+            ri(1, 0, 1)
+            he("V", 4, 0)
+            he("V", 4, 1)
             rq(1, 0, 0)
             rq(1, 0, 1)
+            ml(0)
             hq(4)
-            h_mm(6, 0)
-            h_mm(6, 1)
-            he("S", 6, 0)
-            he("S", 6, 1)
-            sig(3)
+            he("V", 5, 0)
+            he("V", 5, 1)
             ml(1)
             hq(5)
-            ml(2)
-            hq(6)
+            h_mm(6, 0)
+            h_mm(6, 1)
             h_mm(7, 0)
             h_mm(7, 1)
+            ri(1, 1, 0)
+            he("S", 6, 0)
+            he("S", 6, 1)
+            ml(2)
+            hq(6)
+            rq(1, 1, 0)
 
             def p_of(t):
                 if t < T:
@@ -378,44 +384,52 @@ def tile_blockshampooadamgraftstep_x1_kernel(tc, l, g, r, m, v, out_0, out_1, ou
                 if t < T:
                     psq(t, 0)
                     psq(t, 1)
-                    stat(t)
             p_of(0)
-            asq(0)
             sums_of(0)
-            ri(1, 1, 0)
-            ri(1, 1, 1)
-            p_of(1)
+            asq(0)
+            p_root(0)
             asq(1)
-            sums_of(1)
             he("S", 7, 0)
             he("S", 7, 1)
-            asq(2)
+            a_root(0)
+            ri(1, 1, 1)
+            den(0)
+            rq(1, 1, 1)
+            inv(0)
             ml(3)
+            hq(7)
+            fac(0)
+            p_of(1)
+            sums_of(1)
+            asq(2)
             for t in range(T):
                 p_of(t + 2)
+                if t >= 1:
+                    oe("S", t - 1)
+                if t + 1 < T:
+                    p_root(t + 1)
                 fin(t, 0)
                 fin(t, 1)
                 store(t)
-                if t == 0:
-                    rq(1, 1, 0)
-                    rq(1, 1, 1)
-                    hq(7)
-                if t >= 1:
-                    oe_half("S", t - 1, 0)
-                    oe_half("V", t - 1, 1)
+                if t + 1 < T:
+                    den(t + 1)
                 cast(t, 0)
+                if t + 1 < T:
+                    inv(t + 1)
                 cast(t, 1)
                 o_turn(t, 0)
                 o_turn(t, 1)
-                if t + 4 < T:
-                    sig(t + 4)
                 if t + 3 < T:
                     asq(t + 3)
                 sums_of(t + 2)
+                if t + 3 < T and t % 2 == 0:
+                    a_root(t + 2)
                 if t >= 1:
                     oq(t - 1, 0)
                     oq(t - 1, 1)
                     store_words(t - 1)
+                if t + 1 < T:
+                    fac(t + 1)
                 if t == RT:
                     store_scales(0)
                 if t + 4 < T:

@@ -97,24 +97,23 @@ def tile_blockshampooadamgraftstep_x1_kernel(tc, l, g, r, m, v, out_0, out_1, ou
             t = work.tile([P, KP * PACK], BF16, name="g_il", bufs=2, align_bytes=64)
             g_il[b, q] = t
             nc.vector.tensor_copy(
-                out=t[:].rearrange("p (t m j) -> p t m j", t=PACK, j=PACK),
-                in_=g_raw[b, q][:].rearrange("p j (m t) -> p t m j", t=PACK))
+                out=t[:].rearrange("p (t m i j) -> p m t i j", t=PACK, i=2, j=PACK),
+                in_=g_raw[b, q][:].rearrange("p j (m i t) -> p m t i j", i=2, t=PACK))
 
         def gq(b, q):
             i = b * G + q
             nc.vector.quantize_mx(out=g_codes[i][:].bitcast(X4), scales=g_scales[i][:], in_=g_il[b, q][:])
 
-        def ri(b, q, h):
-            t = work.tile([P, 512 * PACK], BF16, name="r_il", bufs=3, align_bytes=64)
-            r_il[b, q, h] = t
+        def ri(b, q):
+            t = work.tile([P, N * PACK], BF16, name="r_il", bufs=2, align_bytes=64)
+            r_il[b, q] = t
             nc.vector.tensor_copy(
                 out=t[:].rearrange("p (c i j) -> p c j i", i=4, j=PACK),
-                in_=r_raw[b, q][:, :, h * 512:(h + 1) * 512].rearrange("p j (c i) -> p c j i", i=4))
+                in_=r_raw[b, q][:].rearrange("p j (c i) -> p c j i", i=4))
 
-        def rq(b, q, h):
+        def rq(b, q):
             i = b * G + q
-            cols = slice(h * 512, (h + 1) * 512)
-            nc.vector.quantize_mx(out=r_codes[i][:, cols].bitcast(X4), scales=r_scales[i][:, cols], in_=r_il[b, q, h][:])
+            nc.vector.quantize_mx(out=r_codes[i][:].bitcast(X4), scales=r_scales[i][:], in_=r_il[b, q][:])
 
         tr_bank = {}
 
@@ -227,12 +226,17 @@ def tile_blockshampooadamgraftstep_x1_kernel(tc, l, g, r, m, v, out_0, out_1, ou
             b, rs = rows(t)
             nc.sync.dma_start(out=out_0[b, rs, :], in_=o32[t][:])
 
-        def cast(t, h):
+        def store_half(t, h):
+            b, rs = rows(t)
+            cols = slice(h * 512, (h + 1) * 512)
+            nc.sync.dma_start(out=out_0[b, rs, cols], in_=o32[t][:, cols])
+
+        def cast(t, h, eng="V"):
             if h == 0:
                 tile = work.tile([P, N], BF16, name="o16", bufs=3)
                 o16[t] = tile
             cols = slice(h * 512, (h + 1) * 512)
-            nc.vector.tensor_copy(out=o16[t][:, cols], in_=o32[t][:, cols])
+            copy_on(eng, o16[t][:, cols], o32[t][:, cols])
 
         def o_turn(t, q):
             if q == 0:
@@ -310,10 +314,8 @@ def tile_blockshampooadamgraftstep_x1_kernel(tc, l, g, r, m, v, out_0, out_1, ou
             ln(2)
             ln(3)
             ln(4)
-            ri(0, 0, 0)
-            ri(0, 0, 1)
-            rq(0, 0, 0)
-            rq(0, 0, 1)
+            ri(0, 0)
+            rq(0, 0)
             for t in range(RT):
                 if t == 1:
                     h_mm(RT - 1, 0)
@@ -327,14 +329,12 @@ def tile_blockshampooadamgraftstep_x1_kernel(tc, l, g, r, m, v, out_0, out_1, ou
                 if t < 3:
                     ln(5 + t)
                 if t == 0:
-                    ri(0, 1, 0)
+                    ri(0, 1)
                 if t == 1:
-                    ri(0, 1, 1)
                     hq(0)
                 if t == 2:
-                    rq(0, 1, 0)
+                    rq(0, 1)
                     hq(1)
-            rq(0, 1, 1)
             l_turn(1, 0)
             l_turn(1, 1)
             gi(1, 0)
@@ -352,12 +352,10 @@ def tile_blockshampooadamgraftstep_x1_kernel(tc, l, g, r, m, v, out_0, out_1, ou
             h_mm(4, 1)
             h_mm(5, 0)
             h_mm(5, 1)
-            ri(1, 0, 0)
-            ri(1, 0, 1)
+            ri(1, 0)
             he("V", 4, 0)
             he("V", 4, 1)
-            rq(1, 0, 0)
-            rq(1, 0, 1)
+            rq(1, 0)
             ml(0)
             hq(4)
             he("V", 5, 0)
@@ -368,12 +366,12 @@ def tile_blockshampooadamgraftstep_x1_kernel(tc, l, g, r, m, v, out_0, out_1, ou
             h_mm(6, 1)
             h_mm(7, 0)
             h_mm(7, 1)
-            ri(1, 1, 0)
+            ri(1, 1)
             he("S", 6, 0)
             he("S", 6, 1)
             ml(2)
             hq(6)
-            rq(1, 1, 0)
+            rq(1, 1)
 
             def p_of(t):
                 if t < T:
@@ -392,9 +390,7 @@ def tile_blockshampooadamgraftstep_x1_kernel(tc, l, g, r, m, v, out_0, out_1, ou
             he("S", 7, 0)
             he("S", 7, 1)
             a_root(0)
-            ri(1, 1, 1)
             den(0)
-            rq(1, 1, 1)
             inv(0)
             ml(3)
             hq(7)
@@ -402,20 +398,17 @@ def tile_blockshampooadamgraftstep_x1_kernel(tc, l, g, r, m, v, out_0, out_1, ou
             p_of(1)
             sums_of(1)
             asq(2)
-            for t in range(T):
+            for t in range(T - 2):
                 p_of(t + 2)
                 if t >= 1:
                     oe("S", t - 1)
-                if t + 1 < T:
-                    p_root(t + 1)
+                p_root(t + 1)
                 fin(t, 0)
                 fin(t, 1)
                 store(t)
-                if t + 1 < T:
-                    den(t + 1)
+                den(t + 1)
                 cast(t, 0)
-                if t + 1 < T:
-                    inv(t + 1)
+                inv(t + 1)
                 cast(t, 1)
                 o_turn(t, 0)
                 o_turn(t, 1)
@@ -428,12 +421,38 @@ def tile_blockshampooadamgraftstep_x1_kernel(tc, l, g, r, m, v, out_0, out_1, ou
                     oq(t - 1, 0)
                     oq(t - 1, 1)
                     store_words(t - 1)
-                if t + 1 < T:
-                    fac(t + 1)
+                fac(t + 1)
                 if t == RT:
                     store_scales(0)
                 if t + 4 < T:
                     ml(t + 4)
+            p_root(T - 1)
+            oe("S", T - 3)
+            fin(T - 2, 0)
+            cast(T - 2, 0, "S")
+            fin(T - 2, 1)
+            store(T - 2)
+            cast(T - 2, 1, "S")
+            den(T - 1)
+            oq(T - 3, 0)
+            inv(T - 1)
+            oq(T - 3, 1)
+            store_words(T - 3)
+            fac(T - 1)
+            o_turn(T - 2, 0)
+            o_turn(T - 2, 1)
+            fin(T - 1, 0)
+            store_half(T - 1, 0)
+            fin(T - 1, 1)
+            store_half(T - 1, 1)
+            cast(T - 1, 0, "S")
+            oe("S", T - 2)
+            cast(T - 1, 1)
+            o_turn(T - 1, 0)
+            o_turn(T - 1, 1)
+            oq(T - 2, 0)
+            oq(T - 2, 1)
+            store_words(T - 2)
             oe_half("S", T - 1, 0)
             oe_half("V", T - 1, 1)
             oq(T - 1, 0)

@@ -8,19 +8,20 @@ BF16 = mybir.dt.bfloat16
 U32 = mybir.dt.uint32
 I32 = mybir.dt.int32
 U8 = mybir.dt.uint8
-X4 = mybir.dt.float8_e4m3fn_x4
+FP8X4 = mybir.dt.float8_e4m3fn_x4
 ACT = mybir.ActivationFunctionType
 ALU = mybir.AluOpType
 
-B, M, N = 2, 512, 1024
-FLOPS = 2 * B * (M * M * N + M * N * N)
+BLOCKS, M, N = 2, 512, 1024
+FLOPS = 2 * BLOCKS * (M * M * N + M * N * N)
+
 P = 128
 PACK = 4
-KP = P * PACK
-G = N // KP
-H = N // 512
-RT = M // P
-T = B * RT
+K_PASS = P * PACK
+GROUPS = N // K_PASS
+HALF = 512
+ROW_TILES = M // P
+TILES = BLOCKS * ROW_TILES
 
 
 def tile_blockshampooadamgraftstep_x1_kernel(tc, l, g, r, m, v, out_0, out_1, out_2):
@@ -28,434 +29,399 @@ def tile_blockshampooadamgraftstep_x1_kernel(tc, l, g, r, m, v, out_0, out_1, ou
     with ExitStack() as ctx:
         keep = ctx.enter_context(tc.tile_pool(name="keep", bufs=1))
         work = ctx.enter_context(tc.tile_pool(name="work", bufs=3))
-        psum = ctx.enter_context(tc.psum_pool(name="psum", bufs=6))
-        psum_t = ctx.enter_context(tc.psum_pool(name="psum_t", bufs=2))
+        product_banks = ctx.enter_context(tc.psum_pool(name="product_banks", bufs=6))
+        turn_banks = ctx.enter_context(tc.psum_pool(name="turn_banks", bufs=2))
 
-        ident = keep.tile([P, P], F32, name="ident")
-        junk = keep.tile([P, N], BF16, name="junk")
-
-        def keep_tiles(name, count, shape, dtype):
+        def kept(name, count, shape, dtype):
             return [keep.tile(shape, dtype, name=name + str(i), align_bytes=64) for i in range(count)]
 
-        v_raw = keep_tiles("v_raw", T, [P, N], BF16)
-        m_raw = keep_tiles("m_raw", T, [P, N], BF16)
-        u = keep_tiles("u", T, [P, N], F32)
-        l_raw = keep_tiles("l_raw", B, [P, RT, M], BF16)
-        l_il = keep_tiles("l_il", B, [P, M * PACK], BF16)
-        l_codes = keep_tiles("l_codes", B, [P, M], U32)
-        l_scales = keep_tiles("l_scales", B, [P, M], U8)
-        g_codes = keep_tiles("g_codes", B * G, [P, KP], U32)
-        g_scales = keep_tiles("g_scales", B * G, [P, KP], U8)
-        r_codes = keep_tiles("r_codes", B * G, [P, N], U32)
-        r_scales = keep_tiles("r_scales", B * G, [P, N], U8)
-        h_codes = keep_tiles("h_codes", T, [P, G * P], U32)
-        h_scales = keep_tiles("h_scales", T, [P, G * P], U8)
-        o_codes = keep_tiles("o_codes", T, [P, G, P], U32)
-        o_scales = keep_tiles("o_scales", B, [P, G, M], U8)
-        p_sums = keep.tile([P, 2 * T], F32, name="p_sums")
-        a_sums = keep.tile([P, T], F32, name="a_sums")
-        p_norms = keep.tile([P, T], F32, name="p_norms")
-        a_norms = keep.tile([P, T], F32, name="a_norms")
-        dens = keep.tile([P, T], F32, name="dens")
-        invs = keep.tile([P, T], F32, name="invs")
-        factors = keep.tile([P, T], F32, name="factors")
+        identity = keep.tile([P, P], F32, name="identity")
+        squares_sink = keep.tile([P, N], BF16, name="squares_sink")
+        v_raw = kept("v_raw", TILES // 2, [P, 2, N], BF16)
+        m_raw = kept("m_raw", TILES // 2, [P, 2, N], BF16)
+        adam = kept("adam", TILES // 2, [P, 2, N], F32)
+        l_raw = kept("l_raw", BLOCKS, [P, ROW_TILES, M], BF16)
+        l_grouped = kept("l_grouped", BLOCKS, [P, M * PACK], BF16)
+        l_codes = kept("l_codes", BLOCKS, [P, M], U32)
+        l_scales = kept("l_scales", BLOCKS, [P, M], U8)
+        g_codes = kept("g_codes", BLOCKS * GROUPS, [P, K_PASS], U32)
+        g_scales = kept("g_scales", BLOCKS * GROUPS, [P, K_PASS], U8)
+        r_codes = kept("r_codes", BLOCKS * GROUPS, [P, N], U32)
+        r_scales = kept("r_scales", BLOCKS * GROUPS, [P, N], U8)
+        h_codes = kept("h_codes", TILES // 2, [P, 2 * GROUPS * P], U32)
+        h_scales = kept("h_scales", TILES // 2, [P, 2 * GROUPS * P], U8)
+        out_codes = kept("out_codes", TILES, [P, GROUPS, P], U32)
+        out_scales = kept("out_scales", BLOCKS, [P, GROUPS, M], U8)
+        p_sums = keep.tile([P, 2 * TILES], F32, name="p_sums")
+        a_sums = keep.tile([P, TILES], F32, name="a_sums")
+        p_norms = keep.tile([P, TILES], F32, name="p_norms")
+        a_norms = keep.tile([P, TILES], F32, name="a_norms")
+        divisors = keep.tile([P, TILES], F32, name="divisors")
+        inverses = keep.tile([P, TILES], F32, name="inverses")
+        factors = keep.tile([P, TILES], F32, name="factors")
 
-        words_out = out_1.bitcast(I32).rearrange("g p m o -> p g (m o)")
-        scales_out = out_2.bitcast(I32)
+        words_hbm = out_1.bitcast(I32).rearrange("g p m o -> p g (m o)")
+        scales_hbm = out_2.bitcast(I32)
 
-        def rows(t):
-            return t // RT, slice((t % RT) * P, (t % RT + 1) * P)
+        def block_rows(t):
+            return t // ROW_TILES, slice((t % ROW_TILES) * P, (t % ROW_TILES + 1) * P)
 
-        def load_v(t):
-            b, rs = rows(t)
-            nc.sync.dma_start(out=v_raw[t][:], in_=v[b, rs, :])
+        def half_cols(h):
+            return slice(h * HALF, (h + 1) * HALF)
 
-        def load_m(t):
-            b, rs = rows(t)
-            nc.sync.dma_start(out=m_raw[t][:], in_=m[b, rs, :])
+        def adam_of(t):
+            return adam[t // 2][:, t % 2, :]
 
-        def load_l(b):
-            nc.sync.dma_start(out=l_raw[b][:], in_=l[b].rearrange("(i p) k -> p i k", p=P))
-
-        g_raw = {}
-        r_raw = {}
-
-        def load_g(b, q):
-            t = work.tile([P, PACK, KP], BF16, name="g_raw", bufs=4, align_bytes=64)
-            g_raw[b, q] = t
-            nc.sync.dma_start(out=t[:], in_=g[b, :, q * KP:(q + 1) * KP].rearrange("(p j) n -> p j n", j=PACK))
-
-        def load_r(b, q):
-            t = work.tile([P, PACK, N], BF16, name="r_raw", bufs=3, align_bytes=64)
-            r_raw[b, q] = t
-            nc.sync.dma_start(out=t[:], in_=r[b, q * KP:(q + 1) * KP, :].rearrange("(p j) n -> p j n", j=PACK))
-
-        g_il = {}
-        r_il = {}
-
-        def gi(b, q):
-            t = work.tile([P, KP * PACK], BF16, name="g_il", bufs=2, align_bytes=64)
-            g_il[b, q] = t
-            nc.vector.tensor_copy(
-                out=t[:].rearrange("p (t m i j) -> p m t i j", t=PACK, i=2, j=PACK),
-                in_=g_raw[b, q][:].rearrange("p j (m i t) -> p m t i j", i=2, t=PACK))
-
-        def gq(b, q):
-            i = b * G + q
-            nc.vector.quantize_mx(out=g_codes[i][:].bitcast(X4), scales=g_scales[i][:], in_=g_il[b, q][:])
-
-        def ri(b, q):
-            t = work.tile([P, N * PACK], BF16, name="r_il", bufs=2, align_bytes=64)
-            r_il[b, q] = t
-            nc.vector.tensor_copy(
-                out=t[:].rearrange("p (c i j) -> p c j i", i=4, j=PACK),
-                in_=r_raw[b, q][:].rearrange("p j (c i) -> p c j i", i=4))
-
-        def rq(b, q):
-            i = b * G + q
-            nc.vector.quantize_mx(out=r_codes[i][:].bitcast(X4), scales=r_scales[i][:], in_=r_il[b, q][:])
-
-        tr_bank = {}
-
-        def l_turn(b, s):
-            bank = psum_t.tile([P, 2, 2, P], F32, name="tr")
-            tr_bank["l", b, s] = bank
-            for i in range(2):
-                words = l_raw[b][:, 2 * s + i, :].bitcast(F32)
-                for w in range(2):
-                    nc.tensor.transpose(out=bank[:, i, w, :], in_=words[:, w::2], identity=ident[:])
-
-        def copy_on(eng, out, in_):
-            if eng == "V":
+        def copy_on(engine, out, in_):
+            if engine == "vector":
                 nc.vector.tensor_copy(out=out, in_=in_)
             else:
                 nc.scalar.copy(out=out, in_=in_)
 
-        def le(eng, b, s):
-            copy_on(eng, l_il[b][:].bitcast(F32)[:, s * 512:(s + 1) * 512].rearrange("p (i r w) -> p i r w", i=2, w=2),
-                    tr_bank["l", b, s][:].rearrange("p i w r -> p i r w"))
+        g_raw, g_grouped, r_raw, r_grouped = {}, {}, {}, {}
+        l_bank, h_bank, h_grouped, p_bank = {}, {}, {}, {}
+        out_f32, out_bf16, out_bank, out_grouped = {}, {}, {}, {}
 
-        def lq(b):
-            nc.vector.quantize_mx(out=l_codes[b][:].bitcast(X4), scales=l_scales[b][:], in_=l_il[b][:])
+        def load_tile(raw, hbm, t):
+            b, rows = block_rows(t)
+            nc.sync.dma_start(out=raw[t // 2][:, t % 2, :], in_=hbm[b, rows, :])
 
-        h_bank = {}
-        h_il = {}
+        def load_pair(raw, hbm, k):
+            b = 2 * k // ROW_TILES
+            start = (2 * k % ROW_TILES) * P
+            nc.sync.dma_start(out=raw[k][:], in_=hbm[b, start:start + 2 * P, :].rearrange("(i p) n -> p i n", p=P))
 
-        def h_mm(t, q):
-            b, i = t // RT, b_g(t, q)
-            bank = psum.tile([P, PACK, P], F32, name="bank")
-            h_bank[t, q] = bank
-            cols = rows(t)[1]
-            for k in range(PACK):
-                sc = slice(k * P, (k + 1) * P)
-                nc.tensor.matmul_mx(out=bank[:, k, :], lhsT=g_codes[i][:, sc].bitcast(X4), lhsT_scale=g_scales[i][:, sc],
-                                    rhs=l_codes[b][:, cols].bitcast(X4), rhs_scale=l_scales[b][:, cols], start=True, stop=True)
+        def load_l(b):
+            nc.sync.dma_start(out=l_raw[b][:], in_=l[b].rearrange("(i p) k -> p i k", p=P))
 
-        def b_g(t, q):
-            return (t // RT) * G + q
+        def load_g(b, q):
+            tile = work.tile([P, PACK, K_PASS], BF16, name="g_raw", bufs=4, align_bytes=64)
+            g_raw[b, q] = tile
+            cols = slice(q * K_PASS, (q + 1) * K_PASS)
+            nc.sync.dma_start(out=tile[:], in_=g[b, :, cols].rearrange("(p j) n -> p j n", j=PACK))
 
-        def he(eng, t, q):
-            if q == 0:
-                tile = work.tile([P, G, P, PACK], BF16, name="h_il", bufs=3, align_bytes=64)
-                h_il[t] = tile
-            copy_on(eng, h_il[t][:, q, :, :], h_bank[t, q][:].rearrange("p t i -> p i t"))
+        def load_r(b, q):
+            tile = work.tile([P, PACK, N], BF16, name="r_raw", bufs=3, align_bytes=64)
+            r_raw[b, q] = tile
+            rows = slice(q * K_PASS, (q + 1) * K_PASS)
+            nc.sync.dma_start(out=tile[:], in_=r[b, rows, :].rearrange("(p j) n -> p j n", j=PACK))
 
-        def hq(t):
-            nc.vector.quantize_mx(out=h_codes[t][:].bitcast(X4), scales=h_scales[t][:],
-                                  in_=h_il[t][:].rearrange("p q i t -> p (q i t)"))
+        def group_g(b, q):
+            tile = work.tile([P, K_PASS * PACK], BF16, name="g_grouped", bufs=2, align_bytes=64)
+            g_grouped[b, q] = tile
+            nc.vector.tensor_copy(
+                out=tile[:].rearrange("p (t m i j) -> p m t j i", t=PACK, i=2, j=PACK),
+                in_=g_raw[b, q][:].rearrange("p j (m i t) -> p m t j i", i=2, t=PACK))
 
-        p_bank = {}
+        def quantize_g(b, q):
+            i = b * GROUPS + q
+            nc.vector.quantize_mx(out=g_codes[i][:].bitcast(FP8X4), scales=g_scales[i][:], in_=g_grouped[b, q][:])
 
-        def p_mm(t, h):
-            bank = psum.tile([P, 512], F32, name="bank")
-            p_bank[t, h] = bank
-            cols = slice(h * 512, (h + 1) * 512)
-            for q in range(G):
-                hs = slice(q * P, (q + 1) * P)
-                i = b_g(t, q)
-                nc.tensor.matmul_mx(out=bank[:], lhsT=h_codes[t][:, hs].bitcast(X4), lhsT_scale=h_scales[t][:, hs],
-                                    rhs=r_codes[i][:, cols].bitcast(X4), rhs_scale=r_scales[i][:, cols],
-                                    start=(q == 0), stop=(q == G - 1))
+        def group_r(b, q):
+            tile = work.tile([P, N * PACK], BF16, name="r_grouped", bufs=2, align_bytes=64)
+            r_grouped[b, q] = tile
+            nc.vector.tensor_copy(
+                out=tile[:].rearrange("p (c i j) -> p c j i", i=4, j=PACK),
+                in_=r_raw[b, q][:].rearrange("p j (c i) -> p c j i", i=4))
 
-        def ln(t):
-            nc.scalar.activation(out=u[t][:], in_=v_raw[t][:], func=ACT.Ln, scale=100.0)
+        def quantize_r(b, q):
+            i = b * GROUPS + q
+            nc.vector.quantize_mx(out=r_codes[i][:].bitcast(FP8X4), scales=r_scales[i][:], in_=r_grouped[b, q][:])
 
-        def sig(t):
-            nc.scalar.activation(out=u[t][:], in_=u[t][:], func=ACT.Sigmoid, scale=-0.5)
+        def turn_l(b):
+            for s in range(ROW_TILES // 2):
+                bank = turn_banks.tile([P, 2, 2, P], F32, name="turned")
+                l_bank[b, s] = bank
+                for i in range(2):
+                    words = l_raw[b][:, 2 * s + i, :].bitcast(F32)
+                    for w in range(2):
+                        nc.tensor.transpose(out=bank[:, i, w, :], in_=words[:, w::2], identity=identity[:])
 
-        def ml(t):
-            nc.vector.scalar_tensor_tensor(out=u[t][:], in0=u[t][:], scalar=3.0, in1=m_raw[t][:], op0=ALU.mult, op1=ALU.mult)
+        def copy_l(b):
+            for s in range(ROW_TILES // 2):
+                words = l_grouped[b][:].bitcast(F32)[:, s * 4 * P:(s + 1) * 4 * P]
+                nc.scalar.copy(out=words.rearrange("p (i r w) -> p i r w", i=2, w=2),
+                               in_=l_bank[b, s][:].rearrange("p i w r -> p i r w"))
 
-        def asq(t):
-            nc.scalar.activation(out=junk[:], in_=u[t][:], func=ACT.Square, accum_out=a_sums[:, t:t + 1])
+        def quantize_l(b):
+            nc.vector.quantize_mx(out=l_codes[b][:].bitcast(FP8X4), scales=l_scales[b][:], in_=l_grouped[b][:])
 
-        def psq(t, h):
-            nc.scalar.activation(out=junk[:, h * 512:(h + 1) * 512], in_=p_bank[t, h][:], func=ACT.Square,
-                                 accum_out=p_sums[:, 2 * t + h:2 * t + h + 1])
+        def multiply_h(t):
+            b, rows = block_rows(t)
+            for q in range(GROUPS):
+                i = b * GROUPS + q
+                bank = product_banks.tile([P, PACK, P], F32, name="product")
+                h_bank[t, q] = bank
+                for k in range(PACK):
+                    cols = slice(k * P, (k + 1) * P)
+                    nc.tensor.matmul_mx(out=bank[:, k, :],
+                                        lhsT=g_codes[i][:, cols].bitcast(FP8X4), lhsT_scale=g_scales[i][:, cols],
+                                        rhs=l_codes[b][:, rows].bitcast(FP8X4), rhs_scale=l_scales[b][:, rows],
+                                        start=True, stop=True)
 
-        def a_root(t):
+        def copy_h(engine, t):
+            if t % 2 == 0:
+                tile = work.tile([P, 2, GROUPS, P, PACK], BF16, name="h_grouped", bufs=2, align_bytes=64)
+                h_grouped[t // 2] = tile
+            for q in range(GROUPS):
+                copy_on(engine, h_grouped[t // 2][:, t % 2, q, :, :], h_bank[t, q][:].rearrange("p k r -> p r k"))
+
+        def quantize_h(k):
+            nc.vector.quantize_mx(out=h_codes[k][:].bitcast(FP8X4), scales=h_scales[k][:],
+                                  in_=h_grouped[k][:].rearrange("p i q r k -> p (i q r k)"))
+
+        def multiply_p(t):
+            for h in range(2):
+                bank = product_banks.tile([P, HALF], F32, name="product")
+                p_bank[t, h] = bank
+                for q in range(GROUPS):
+                    i = (t // ROW_TILES) * GROUPS + q
+                    start = ((t % 2) * GROUPS + q) * P
+                    rows = slice(start, start + P)
+                    cols = half_cols(h)
+                    nc.tensor.matmul_mx(out=bank[:],
+                                        lhsT=h_codes[t // 2][:, rows].bitcast(FP8X4), lhsT_scale=h_scales[t // 2][:, rows],
+                                        rhs=r_codes[i][:, cols].bitcast(FP8X4), rhs_scale=r_scales[i][:, cols],
+                                        start=(q == 0), stop=(q == GROUPS - 1))
+
+        def log_v(t):
+            nc.scalar.activation(out=adam_of(t), in_=v_raw[t // 2][:, t % 2, :], func=ACT.Ln, scale=100.0)
+
+        def log_v_pair(k):
+            nc.scalar.activation(out=adam[k][:], in_=v_raw[k][:], func=ACT.Ln, scale=100.0)
+
+        def sigmoid_pair(k):
+            nc.scalar.activation(out=adam[k][:], in_=adam[k][:], func=ACT.Sigmoid, scale=-0.5)
+
+        def times_m(t):
+            nc.vector.scalar_tensor_tensor(out=adam_of(t), in0=adam_of(t), scalar=3.0, in1=m_raw[t // 2][:, t % 2, :],
+                                           op0=ALU.mult, op1=ALU.mult)
+
+        def times_m_pair(k):
+            nc.vector.scalar_tensor_tensor(out=adam[k][:].rearrange("p i n -> p (i n)"), in0=adam[k][:].rearrange("p i n -> p (i n)"),
+                                           scalar=3.0, in1=m_raw[k][:].rearrange("p i n -> p (i n)"), op0=ALU.mult, op1=ALU.mult)
+
+        def square_a(t):
+            nc.scalar.activation(out=squares_sink[:], in_=adam_of(t), func=ACT.Square, accum_out=a_sums[:, t:t + 1])
+
+        def square_p(t):
+            for h in range(2):
+                nc.scalar.activation(out=squares_sink[:, half_cols(h)], in_=p_bank[t, h][:], func=ACT.Square,
+                                     accum_out=p_sums[:, 2 * t + h:2 * t + h + 1])
+
+        def root_a(t):
             nc.scalar.activation(out=a_norms[:, t:t + 2], in_=a_sums[:, t:t + 2], func=ACT.Sqrt, scale=49.0 / 9.0)
 
-        def p_root(t):
+        def root_p(t):
             nc.scalar.activation(out=p_norms[:, t:t + 1], in_=p_sums[:, 2 * t:2 * t + 1], func=ACT.Sqrt,
                                  bias=p_sums[:, 2 * t + 1:2 * t + 2])
 
-        def den(t):
-            nc.vector.tensor_scalar(out=dens[:, t:t + 1], in0=p_norms[:, t:t + 1], scalar1=1e-6, scalar2=None, op0=ALU.add)
+        def divisor(t):
+            nc.vector.tensor_scalar(out=divisors[:, t:t + 1], in0=p_norms[:, t:t + 1], scalar1=1e-6, scalar2=None, op0=ALU.add)
 
-        def inv(t):
-            nc.vector.reciprocal(out=invs[:, t:t + 1], in_=dens[:, t:t + 1])
+        def inverse(t):
+            nc.vector.reciprocal(out=inverses[:, t:t + 1], in_=divisors[:, t:t + 1])
 
-        def fac(t):
-            nc.vector.tensor_scalar(out=factors[:, t:t + 1], in0=invs[:, t:t + 1], scalar1=a_norms[:, t:t + 1], scalar2=None,
-                                    op0=ALU.mult)
+        def factor(t):
+            nc.vector.tensor_scalar(out=factors[:, t:t + 1], in0=inverses[:, t:t + 1], scalar1=a_norms[:, t:t + 1],
+                                    scalar2=None, op0=ALU.mult)
 
-        o32 = {}
-        o16 = {}
-        o_il = {}
-
-        def fin(t, h):
+        def mix(t, h):
             if h == 0:
-                tile = work.tile([P, N], F32, name="o32", bufs=3)
-                o32[t] = tile
-            cols = slice(h * 512, (h + 1) * 512)
-            nc.vector.scalar_tensor_tensor(out=o32[t][:, cols], in0=p_bank[t, h][:], scalar=factors[:, t:t + 1],
-                                           in1=u[t][:, cols], op0=ALU.mult, op1=ALU.add)
+                tile = work.tile([P, N], F32, name="out_f32", bufs=3)
+                out_f32[t] = tile
+            cols = half_cols(h)
+            nc.vector.scalar_tensor_tensor(out=out_f32[t][:, cols], in0=p_bank[t, h][:], scalar=factors[:, t:t + 1],
+                                           in1=adam_of(t)[:, cols], op0=ALU.mult, op1=ALU.add)
 
-        def store(t):
-            b, rs = rows(t)
-            nc.sync.dma_start(out=out_0[b, rs, :], in_=o32[t][:])
+        def store_out(t):
+            b, rows = block_rows(t)
+            nc.sync.dma_start(out=out_0[b, rows, :], in_=out_f32[t][:])
 
-        def store_half(t, h):
-            b, rs = rows(t)
-            cols = slice(h * 512, (h + 1) * 512)
-            nc.sync.dma_start(out=out_0[b, rs, cols], in_=o32[t][:, cols])
+        def store_out_half(t, h):
+            b, rows = block_rows(t)
+            nc.sync.dma_start(out=out_0[b, rows, half_cols(h)], in_=out_f32[t][:, half_cols(h)])
 
-        def cast(t, h, eng="V"):
+        def round_out(engine, t, h):
             if h == 0:
-                tile = work.tile([P, N], BF16, name="o16", bufs=3)
-                o16[t] = tile
-            cols = slice(h * 512, (h + 1) * 512)
-            copy_on(eng, o16[t][:, cols], o32[t][:, cols])
+                tile = work.tile([P, N], BF16, name="out_bf16", bufs=2)
+                out_bf16[t] = tile
+            copy_on(engine, out_bf16[t][:, half_cols(h)], out_f32[t][:, half_cols(h)])
 
-        def o_turn(t, q):
+        def turn_out(t):
+            bank = turn_banks.tile([P, GROUPS, 2, P], F32, name="turned")
+            out_bank[t] = bank
+            words = out_bf16[t][:].bitcast(F32)
+            for q in range(GROUPS):
+                for w in range(2):
+                    nc.tensor.transpose(out=bank[:, q, w, :], in_=words[:, q * 2 * P + w:(q + 1) * 2 * P:2], identity=identity[:])
+
+        def grouped_tile(t):
+            tile = work.tile([P, GROUPS * P * PACK], BF16, name="out_grouped", bufs=3, align_bytes=64)
+            out_grouped[t] = tile
+
+        def copy_out(t):
+            grouped_tile(t)
+            nc.scalar.copy(out=out_grouped[t][:].bitcast(F32).rearrange("p (q r w) -> p q r w", q=GROUPS, w=2),
+                           in_=out_bank[t][:].rearrange("p q w r -> p q r w"))
+
+        def copy_out_group(engine, t, q):
             if q == 0:
-                bank = psum_t.tile([P, G, 2, P], F32, name="tr")
-                tr_bank["o", t] = bank
-            words = o16[t][:].bitcast(F32)
-            for w in range(2):
-                nc.tensor.transpose(out=tr_bank["o", t][:, q, w, :], in_=words[:, q * 256 + w:(q + 1) * 256:2], identity=ident[:])
+                grouped_tile(t)
+            copy_on(engine, out_grouped[t][:].bitcast(F32)[:, q * 2 * P:(q + 1) * 2 * P].rearrange("p (r w) -> p r w", w=2),
+                    out_bank[t][:, q, :, :].rearrange("p w r -> p r w"))
 
-        def oe_tile(t):
-            tile = work.tile([P, G * P * PACK], BF16, name="o_il", bufs=3, align_bytes=64)
-            o_il[t] = tile
-
-        def oe(eng, t):
-            oe_tile(t)
-            copy_on(eng, o_il[t][:].bitcast(F32).rearrange("p (q r w) -> p q r w", q=G, w=2),
-                    tr_bank["o", t][:].rearrange("p q w r -> p q r w"))
-
-        def oe_half(eng, t, q):
-            if q == 0:
-                oe_tile(t)
-            copy_on(eng, o_il[t][:].bitcast(F32)[:, q * 256:(q + 1) * 256].rearrange("p (r w) -> p r w", w=2),
-                    tr_bank["o", t][:, q, :, :].rearrange("p w r -> p r w"))
-
-        def oq(t, q):
-            b, rs = rows(t)
-            nc.vector.quantize_mx(out=o_codes[t][:, q, :].bitcast(X4), scales=o_scales[b][:, q, rs],
-                                  in_=o_il[t][:, q * 512:(q + 1) * 512])
+        def quantize_out(t):
+            b, rows = block_rows(t)
+            for q in range(GROUPS):
+                nc.vector.quantize_mx(out=out_codes[t][:, q, :].bitcast(FP8X4), scales=out_scales[b][:, q, rows],
+                                      in_=out_grouped[t][:, q * K_PASS:(q + 1) * K_PASS])
 
         def store_words(t):
-            nc.sync.dma_start(out=words_out[:, :, t * P:(t + 1) * P], in_=o_codes[t][:].bitcast(I32))
+            nc.sync.dma_start(out=words_hbm[:, :, t * P:(t + 1) * P], in_=out_codes[t][:].bitcast(I32))
 
         def store_scales(b):
-            for q in range(4):
+            for k in range(4):
                 nc.sync.dma_start(
-                    out=scales_out[:, 4 * q:4 * q + 4, b * P:(b + 1) * P].rearrange("g r m -> r g m"),
-                    in_=o_scales[b][32 * q:32 * q + 4, :, :].bitcast(I32))
+                    out=scales_hbm[:, 4 * k:4 * k + 4, b * P:(b + 1) * P].rearrange("g r m -> r g m"),
+                    in_=out_scales[b][32 * k:32 * k + 4, :, :].bitcast(I32))
 
         with tc.manual_schedule():
-            make_identity(nc, ident[:])
+            make_identity(nc, identity[:])
             load_g(0, 0)
-            load_v(0)
-            load_v(1)
+            load_tile(v_raw, v, 0)
+            load_tile(v_raw, v, 1)
             load_l(0)
             load_g(0, 1)
-            load_v(2)
-            load_v(3)
+            load_pair(v_raw, v, 1)
             load_r(0, 0)
-            load_v(4)
-            load_v(5)
+            load_pair(v_raw, v, 2)
             load_r(0, 1)
-            load_v(6)
-            load_v(7)
+            load_pair(v_raw, v, 3)
             load_g(1, 0)
             load_l(1)
             load_g(1, 1)
             load_r(1, 0)
-            load_m(0)
-            load_m(1)
+            load_pair(m_raw, m, 0)
 
-            ln(0)
-            gi(0, 0)
-            l_turn(0, 0)
-            l_turn(0, 1)
-            ln(1)
-            gq(0, 0)
-            le("S", 0, 0)
-            le("S", 0, 1)
-            gi(0, 1)
-            lq(0)
-            gq(0, 1)
-            for t in range(RT - 1):
-                h_mm(t, 0)
-                h_mm(t, 1)
-            ln(2)
-            ln(3)
-            ln(4)
-            ri(0, 0)
-            rq(0, 0)
-            for t in range(RT):
-                if t == 1:
-                    h_mm(RT - 1, 0)
-                    h_mm(RT - 1, 1)
-                he("S", t, 0)
-                he("S", t, 1)
-                if t == 0:
-                    load_r(1, 1)
-                    for k in range(2, T):
-                        load_m(k)
-                if t < 3:
-                    ln(5 + t)
-                if t == 0:
-                    ri(0, 1)
-                if t == 1:
-                    hq(0)
-                if t == 2:
-                    rq(0, 1)
-                    hq(1)
-            l_turn(1, 0)
-            l_turn(1, 1)
-            gi(1, 0)
-            hq(2)
-            le("S", 1, 0)
-            le("S", 1, 1)
-            gq(1, 0)
-            gi(1, 1)
-            hq(3)
-            lq(1)
-            gq(1, 1)
-            for t in range(T):
-                sig(t)
-            h_mm(4, 0)
-            h_mm(4, 1)
-            h_mm(5, 0)
-            h_mm(5, 1)
-            ri(1, 0)
-            he("V", 4, 0)
-            he("V", 4, 1)
-            rq(1, 0)
-            ml(0)
-            hq(4)
-            he("V", 5, 0)
-            he("V", 5, 1)
-            ml(1)
-            hq(5)
-            h_mm(6, 0)
-            h_mm(6, 1)
-            h_mm(7, 0)
-            h_mm(7, 1)
-            ri(1, 1)
-            he("S", 6, 0)
-            he("S", 6, 1)
-            ml(2)
-            hq(6)
-            rq(1, 1)
-
-            def p_of(t):
-                if t < T:
-                    p_mm(t, 0)
-                    p_mm(t, 1)
-
-            def sums_of(t):
-                if t < T:
-                    psq(t, 0)
-                    psq(t, 1)
-            p_of(0)
-            sums_of(0)
-            asq(0)
-            p_root(0)
-            asq(1)
-            he("S", 7, 0)
-            he("S", 7, 1)
-            a_root(0)
-            den(0)
-            inv(0)
-            ml(3)
-            hq(7)
-            fac(0)
-            p_of(1)
-            sums_of(1)
-            asq(2)
-            for t in range(T - 2):
-                p_of(t + 2)
+            log_v(0)
+            group_g(0, 0)
+            turn_l(0)
+            log_v(1)
+            quantize_g(0, 0)
+            copy_l(0)
+            group_g(0, 1)
+            quantize_l(0)
+            quantize_g(0, 1)
+            multiply_h(0)
+            multiply_h(1)
+            multiply_h(2)
+            log_v_pair(1)
+            group_r(0, 0)
+            load_r(1, 1)
+            for k in range(1, TILES // 2):
+                load_pair(m_raw, m, k)
+            copy_h("scalar", 0)
+            multiply_h(3)
+            log_v_pair(2)
+            copy_h("scalar", 1)
+            quantize_r(0, 0)
+            group_r(0, 1)
+            copy_h("scalar", 2)
+            quantize_h(0)
+            quantize_r(0, 1)
+            log_v_pair(3)
+            turn_l(1)
+            copy_h("scalar", 3)
+            group_g(1, 0)
+            copy_l(1)
+            quantize_h(1)
+            quantize_g(1, 0)
+            group_g(1, 1)
+            quantize_l(1)
+            quantize_g(1, 1)
+            for k in range(TILES // 2):
+                sigmoid_pair(k)
+            multiply_h(4)
+            multiply_h(5)
+            group_r(1, 0)
+            copy_h("vector", 4)
+            quantize_r(1, 0)
+            copy_h("vector", 5)
+            times_m_pair(0)
+            quantize_h(2)
+            multiply_h(6)
+            multiply_h(7)
+            group_r(1, 1)
+            copy_h("scalar", 6)
+            times_m_pair(1)
+            multiply_p(0)
+            square_p(0)
+            square_a(0)
+            root_p(0)
+            square_a(1)
+            copy_h("scalar", 7)
+            root_a(0)
+            divisor(0)
+            quantize_r(1, 1)
+            inverse(0)
+            quantize_h(3)
+            factor(0)
+            multiply_p(1)
+            square_p(1)
+            square_a(2)
+            for t in range(TILES - 2):
+                multiply_p(t + 2)
                 if t >= 1:
-                    oe("S", t - 1)
-                p_root(t + 1)
-                fin(t, 0)
-                fin(t, 1)
-                store(t)
-                den(t + 1)
-                cast(t, 0)
-                inv(t + 1)
-                cast(t, 1)
-                o_turn(t, 0)
-                o_turn(t, 1)
-                if t + 3 < T:
-                    asq(t + 3)
-                sums_of(t + 2)
-                if t + 3 < T and t % 2 == 0:
-                    a_root(t + 2)
+                    copy_out(t - 1)
+                root_p(t + 1)
+                mix(t, 0)
+                mix(t, 1)
+                store_out(t)
+                divisor(t + 1)
+                round_out("vector", t, 0)
+                inverse(t + 1)
+                round_out("vector", t, 1)
+                turn_out(t)
+                if t + 3 < TILES:
+                    square_a(t + 3)
+                square_p(t + 2)
+                if t % 2 == 0 and t + 3 < TILES:
+                    root_a(t + 2)
                 if t >= 1:
-                    oq(t - 1, 0)
-                    oq(t - 1, 1)
+                    quantize_out(t - 1)
                     store_words(t - 1)
-                fac(t + 1)
-                if t == RT:
+                factor(t + 1)
+                if t == ROW_TILES:
                     store_scales(0)
-                if t + 4 < T:
-                    ml(t + 4)
-            p_root(T - 1)
-            oe("S", T - 3)
-            fin(T - 2, 0)
-            cast(T - 2, 0, "S")
-            fin(T - 2, 1)
-            store(T - 2)
-            cast(T - 2, 1, "S")
-            den(T - 1)
-            oq(T - 3, 0)
-            inv(T - 1)
-            oq(T - 3, 1)
-            store_words(T - 3)
-            fac(T - 1)
-            o_turn(T - 2, 0)
-            o_turn(T - 2, 1)
-            fin(T - 1, 0)
-            store_half(T - 1, 0)
-            fin(T - 1, 1)
-            store_half(T - 1, 1)
-            cast(T - 1, 0, "S")
-            oe("S", T - 2)
-            cast(T - 1, 1)
-            o_turn(T - 1, 0)
-            o_turn(T - 1, 1)
-            oq(T - 2, 0)
-            oq(T - 2, 1)
-            store_words(T - 2)
-            oe_half("S", T - 1, 0)
-            oe_half("V", T - 1, 1)
-            oq(T - 1, 0)
-            oq(T - 1, 1)
-            store_words(T - 1)
+                if t + 4 < TILES:
+                    times_m(t + 4)
+            a, b, c = TILES - 3, TILES - 2, TILES - 1
+            root_p(c)
+            copy_out(a)
+            mix(b, 0)
+            round_out("scalar", b, 0)
+            mix(b, 1)
+            store_out(b)
+            round_out("scalar", b, 1)
+            divisor(c)
+            quantize_out(a)
+            store_words(a)
+            inverse(c)
+            factor(c)
+            turn_out(b)
+            mix(c, 0)
+            store_out_half(c, 0)
+            mix(c, 1)
+            store_out_half(c, 1)
+            round_out("scalar", c, 0)
+            copy_out(b)
+            round_out("vector", c, 1)
+            turn_out(c)
+            quantize_out(b)
+            store_words(b)
+            copy_out_group("scalar", c, 0)
+            copy_out_group("vector", c, 1)
+            quantize_out(c)
+            store_words(c)
             store_scales(1)

from contextlib import ExitStack

import concourse.mybir as mybir
from concourse.masks import make_identity

F32 = mybir.dt.float32
BF16 = mybir.dt.bfloat16
U32 = mybir.dt.uint32
I32 = mybir.dt.int32
U8 = mybir.dt.uint8
FP8X4 = mybir.dt.float8_e4m3fn_x4
ACT = mybir.ActivationFunctionType
ALU = mybir.AluOpType

BLOCKS, M, N = 2, 512, 1024
FLOPS = 2 * BLOCKS * (M * M * N + M * N * N)

P = 128
PACK = 4
K_PASS = P * PACK
GROUPS = N // K_PASS
HALF = 512
ROW_TILES = M // P
TILES = BLOCKS * ROW_TILES


def tile_blockshampooadamgraftstep_x1_kernel(tc, l, g, r, m, v, out_0, out_1, out_2):
    nc = tc.nc
    with ExitStack() as ctx:
        keep = ctx.enter_context(tc.tile_pool(name="keep", bufs=1))
        work = ctx.enter_context(tc.tile_pool(name="work", bufs=3))
        product_banks = ctx.enter_context(tc.psum_pool(name="product_banks", bufs=6))
        turn_banks = ctx.enter_context(tc.psum_pool(name="turn_banks", bufs=2))

        def kept(name, count, shape, dtype):
            return [keep.tile(shape, dtype, name=name + str(i), align_bytes=64) for i in range(count)]

        identity = keep.tile([P, P], F32, name="identity")
        squares_sink = keep.tile([P, N], BF16, name="squares_sink")
        v_raw = kept("v_raw", TILES // 2, [P, 2, N], BF16)
        m_raw = kept("m_raw", TILES // 2, [P, 2, N], BF16)
        adam = kept("adam", TILES // 2, [P, 2, N], F32)
        l_raw = kept("l_raw", BLOCKS, [P, ROW_TILES, M], BF16)
        l_grouped = kept("l_grouped", BLOCKS, [P, M * PACK], BF16)
        l_codes = kept("l_codes", BLOCKS, [P, M], U32)
        l_scales = kept("l_scales", BLOCKS, [P, M], U8)
        g_codes = kept("g_codes", BLOCKS * GROUPS, [P, K_PASS], U32)
        g_scales = kept("g_scales", BLOCKS * GROUPS, [P, K_PASS], U8)
        r_codes = kept("r_codes", BLOCKS * GROUPS, [P, N], U32)
        r_scales = kept("r_scales", BLOCKS * GROUPS, [P, N], U8)
        h_codes = kept("h_codes", TILES // 2, [P, 2 * GROUPS * P], U32)
        h_scales = kept("h_scales", TILES // 2, [P, 2 * GROUPS * P], U8)
        out_codes = kept("out_codes", TILES, [P, GROUPS, P], U32)
        out_scales = kept("out_scales", BLOCKS, [P, GROUPS, M], U8)
        p_sums = keep.tile([P, 2 * TILES], F32, name="p_sums")
        a_sums = keep.tile([P, TILES], F32, name="a_sums")
        p_norms = keep.tile([P, TILES], F32, name="p_norms")
        a_norms = keep.tile([P, TILES], F32, name="a_norms")
        divisors = keep.tile([P, TILES], F32, name="divisors")
        inverses = keep.tile([P, TILES], F32, name="inverses")
        factors = keep.tile([P, TILES], F32, name="factors")

        words_hbm = out_1.bitcast(I32).rearrange("g p m o -> p g (m o)")
        scales_hbm = out_2.bitcast(I32)

        def block_rows(t):
            return t // ROW_TILES, slice((t % ROW_TILES) * P, (t % ROW_TILES + 1) * P)

        def half_cols(h):
            return slice(h * HALF, (h + 1) * HALF)

        def adam_of(t):
            return adam[t // 2][:, t % 2, :]

        def copy_on(engine, out, in_):
            if engine == "vector":
                nc.vector.tensor_copy(out=out, in_=in_)
            else:
                nc.scalar.copy(out=out, in_=in_)

        g_raw, g_grouped, r_raw, r_grouped = {}, {}, {}, {}
        l_bank, h_bank, h_grouped, p_bank = {}, {}, {}, {}
        out_f32, out_bf16, out_bank, out_grouped = {}, {}, {}, {}

        def load_tile(raw, hbm, t):
            b, rows = block_rows(t)
            nc.sync.dma_start(out=raw[t // 2][:, t % 2, :], in_=hbm[b, rows, :])

        def load_pair(raw, hbm, k):
            b = 2 * k // ROW_TILES
            start = (2 * k % ROW_TILES) * P
            nc.sync.dma_start(out=raw[k][:], in_=hbm[b, start:start + 2 * P, :].rearrange("(i p) n -> p i n", p=P))

        def load_l(b):
            nc.sync.dma_start(out=l_raw[b][:], in_=l[b].rearrange("(i p) k -> p i k", p=P))

        def load_g(b, q):
            tile = work.tile([P, PACK, K_PASS], BF16, name="g_raw", bufs=4, align_bytes=64)
            g_raw[b, q] = tile
            cols = slice(q * K_PASS, (q + 1) * K_PASS)
            nc.sync.dma_start(out=tile[:], in_=g[b, :, cols].rearrange("(p j) n -> p j n", j=PACK))

        def load_r(b, q):
            tile = work.tile([P, PACK, N], BF16, name="r_raw", bufs=3, align_bytes=64)
            r_raw[b, q] = tile
            rows = slice(q * K_PASS, (q + 1) * K_PASS)
            nc.sync.dma_start(out=tile[:], in_=r[b, rows, :].rearrange("(p j) n -> p j n", j=PACK))

        def group_g(b, q):
            tile = work.tile([P, K_PASS * PACK], BF16, name="g_grouped", bufs=2, align_bytes=64)
            g_grouped[b, q] = tile
            nc.vector.tensor_copy(
                out=tile[:].rearrange("p (t m i j) -> p m t j i", t=PACK, i=2, j=PACK),
                in_=g_raw[b, q][:].rearrange("p j (m i t) -> p m t j i", i=2, t=PACK))

        def quantize_g(b, q):
            i = b * GROUPS + q
            nc.vector.quantize_mx(out=g_codes[i][:].bitcast(FP8X4), scales=g_scales[i][:], in_=g_grouped[b, q][:])

        def group_r(b, q):
            tile = work.tile([P, N * PACK], BF16, name="r_grouped", bufs=2, align_bytes=64)
            r_grouped[b, q] = tile
            nc.vector.tensor_copy(
                out=tile[:].rearrange("p (c i j) -> p c j i", i=4, j=PACK),
                in_=r_raw[b, q][:].rearrange("p j (c i) -> p c j i", i=4))

        def quantize_r(b, q):
            i = b * GROUPS + q
            nc.vector.quantize_mx(out=r_codes[i][:].bitcast(FP8X4), scales=r_scales[i][:], in_=r_grouped[b, q][:])

        def turn_l(b):
            for s in range(ROW_TILES // 2):
                bank = turn_banks.tile([P, 2, 2, P], F32, name="turned")
                l_bank[b, s] = bank
                for i in range(2):
                    words = l_raw[b][:, 2 * s + i, :].bitcast(F32)
                    for w in range(2):
                        nc.tensor.transpose(out=bank[:, i, w, :], in_=words[:, w::2], identity=identity[:])

        def copy_l(b):
            for s in range(ROW_TILES // 2):
                words = l_grouped[b][:].bitcast(F32)[:, s * 4 * P:(s + 1) * 4 * P]
                nc.scalar.copy(out=words.rearrange("p (i r w) -> p i r w", i=2, w=2),
                               in_=l_bank[b, s][:].rearrange("p i w r -> p i r w"))

        def quantize_l(b):
            nc.vector.quantize_mx(out=l_codes[b][:].bitcast(FP8X4), scales=l_scales[b][:], in_=l_grouped[b][:])

        def multiply_h(t):
            b, rows = block_rows(t)
            for q in range(GROUPS):
                i = b * GROUPS + q
                bank = product_banks.tile([P, PACK, P], F32, name="product")
                h_bank[t, q] = bank
                for k in range(PACK):
                    cols = slice(k * P, (k + 1) * P)
                    nc.tensor.matmul_mx(out=bank[:, k, :],
                                        lhsT=g_codes[i][:, cols].bitcast(FP8X4), lhsT_scale=g_scales[i][:, cols],
                                        rhs=l_codes[b][:, rows].bitcast(FP8X4), rhs_scale=l_scales[b][:, rows],
                                        start=True, stop=True)

        def copy_h(engine, t):
            if t % 2 == 0:
                tile = work.tile([P, 2, GROUPS, P, PACK], BF16, name="h_grouped", bufs=2, align_bytes=64)
                h_grouped[t // 2] = tile
            for q in range(GROUPS):
                copy_on(engine, h_grouped[t // 2][:, t % 2, q, :, :], h_bank[t, q][:].rearrange("p k r -> p r k"))

        def quantize_h(k):
            nc.vector.quantize_mx(out=h_codes[k][:].bitcast(FP8X4), scales=h_scales[k][:],
                                  in_=h_grouped[k][:].rearrange("p i q r k -> p (i q r k)"))

        def multiply_p(t):
            for h in range(2):
                bank = product_banks.tile([P, HALF], F32, name="product")
                p_bank[t, h] = bank
                for q in range(GROUPS):
                    i = (t // ROW_TILES) * GROUPS + q
                    start = ((t % 2) * GROUPS + q) * P
                    rows = slice(start, start + P)
                    cols = half_cols(h)
                    nc.tensor.matmul_mx(out=bank[:],
                                        lhsT=h_codes[t // 2][:, rows].bitcast(FP8X4), lhsT_scale=h_scales[t // 2][:, rows],
                                        rhs=r_codes[i][:, cols].bitcast(FP8X4), rhs_scale=r_scales[i][:, cols],
                                        start=(q == 0), stop=(q == GROUPS - 1))

        def log_v(t):
            nc.scalar.activation(out=adam_of(t), in_=v_raw[t // 2][:, t % 2, :], func=ACT.Ln, scale=100.0)

        def log_v_pair(k):
            nc.scalar.activation(out=adam[k][:], in_=v_raw[k][:], func=ACT.Ln, scale=100.0)

        def sigmoid_pair(k):
            nc.scalar.activation(out=adam[k][:], in_=adam[k][:], func=ACT.Sigmoid, scale=-0.5)

        def times_m(t):
            nc.vector.scalar_tensor_tensor(out=adam_of(t), in0=adam_of(t), scalar=3.0, in1=m_raw[t // 2][:, t % 2, :],
                                           op0=ALU.mult, op1=ALU.mult)

        def times_m_pair(k):
            nc.vector.scalar_tensor_tensor(out=adam[k][:].rearrange("p i n -> p (i n)"), in0=adam[k][:].rearrange("p i n -> p (i n)"),
                                           scalar=3.0, in1=m_raw[k][:].rearrange("p i n -> p (i n)"), op0=ALU.mult, op1=ALU.mult)

        def square_a(t):
            nc.scalar.activation(out=squares_sink[:], in_=adam_of(t), func=ACT.Square, accum_out=a_sums[:, t:t + 1])

        def square_p(t):
            for h in range(2):
                nc.scalar.activation(out=squares_sink[:, half_cols(h)], in_=p_bank[t, h][:], func=ACT.Square,
                                     accum_out=p_sums[:, 2 * t + h:2 * t + h + 1])

        def root_a(t):
            nc.scalar.activation(out=a_norms[:, t:t + 2], in_=a_sums[:, t:t + 2], func=ACT.Sqrt, scale=49.0 / 9.0)

        def root_p(t):
            nc.scalar.activation(out=p_norms[:, t:t + 1], in_=p_sums[:, 2 * t:2 * t + 1], func=ACT.Sqrt,
                                 bias=p_sums[:, 2 * t + 1:2 * t + 2])

        def divisor(t):
            nc.vector.tensor_scalar(out=divisors[:, t:t + 1], in0=p_norms[:, t:t + 1], scalar1=1e-6, scalar2=None, op0=ALU.add)

        def inverse(t):
            nc.vector.reciprocal(out=inverses[:, t:t + 1], in_=divisors[:, t:t + 1])

        def factor(t):
            nc.vector.tensor_scalar(out=factors[:, t:t + 1], in0=inverses[:, t:t + 1], scalar1=a_norms[:, t:t + 1],
                                    scalar2=None, op0=ALU.mult)

        def mix(t, h):
            if h == 0:
                tile = work.tile([P, N], F32, name="out_f32", bufs=3)
                out_f32[t] = tile
            cols = half_cols(h)
            nc.vector.scalar_tensor_tensor(out=out_f32[t][:, cols], in0=p_bank[t, h][:], scalar=factors[:, t:t + 1],
                                           in1=adam_of(t)[:, cols], op0=ALU.mult, op1=ALU.add)

        def store_out(t):
            b, rows = block_rows(t)
            nc.sync.dma_start(out=out_0[b, rows, :], in_=out_f32[t][:])

        def store_out_half(t, h):
            b, rows = block_rows(t)
            nc.sync.dma_start(out=out_0[b, rows, half_cols(h)], in_=out_f32[t][:, half_cols(h)])

        def round_out(engine, t, h):
            if h == 0:
                tile = work.tile([P, N], BF16, name="out_bf16", bufs=2)
                out_bf16[t] = tile
            copy_on(engine, out_bf16[t][:, half_cols(h)], out_f32[t][:, half_cols(h)])

        def turn_out(t):
            bank = turn_banks.tile([P, GROUPS, 2, P], F32, name="turned")
            out_bank[t] = bank
            words = out_bf16[t][:].bitcast(F32)
            for q in range(GROUPS):
                for w in range(2):
                    nc.tensor.transpose(out=bank[:, q, w, :], in_=words[:, q * 2 * P + w:(q + 1) * 2 * P:2], identity=identity[:])

        def grouped_tile(t):
            tile = work.tile([P, GROUPS * P * PACK], BF16, name="out_grouped", bufs=3, align_bytes=64)
            out_grouped[t] = tile

        def copy_out(t):
            grouped_tile(t)
            nc.scalar.copy(out=out_grouped[t][:].bitcast(F32).rearrange("p (q r w) -> p q r w", q=GROUPS, w=2),
                           in_=out_bank[t][:].rearrange("p q w r -> p q r w"))

        def copy_out_group(engine, t, q):
            if q == 0:
                grouped_tile(t)
            copy_on(engine, out_grouped[t][:].bitcast(F32)[:, q * 2 * P:(q + 1) * 2 * P].rearrange("p (r w) -> p r w", w=2),
                    out_bank[t][:, q, :, :].rearrange("p w r -> p r w"))

        def quantize_out(t):
            b, rows = block_rows(t)
            for q in range(GROUPS):
                nc.vector.quantize_mx(out=out_codes[t][:, q, :].bitcast(FP8X4), scales=out_scales[b][:, q, rows],
                                      in_=out_grouped[t][:, q * K_PASS:(q + 1) * K_PASS])

        def store_words(t):
            nc.sync.dma_start(out=words_hbm[:, :, t * P:(t + 1) * P], in_=out_codes[t][:].bitcast(I32))

        def store_scales(b):
            for k in range(4):
                nc.sync.dma_start(
                    out=scales_hbm[:, 4 * k:4 * k + 4, b * P:(b + 1) * P].rearrange("g r m -> r g m"),
                    in_=out_scales[b][32 * k:32 * k + 4, :, :].bitcast(I32))

        with tc.manual_schedule():
            make_identity(nc, identity[:])
            load_g(0, 0)
            load_tile(v_raw, v, 0)
            load_tile(v_raw, v, 1)
            load_l(0)
            load_g(0, 1)
            load_pair(v_raw, v, 1)
            load_r(0, 0)
            load_pair(v_raw, v, 2)
            load_r(0, 1)
            load_pair(v_raw, v, 3)
            load_g(1, 0)
            load_l(1)
            load_g(1, 1)
            load_r(1, 0)
            load_pair(m_raw, m, 0)

            log_v(0)
            group_g(0, 0)
            turn_l(0)
            log_v(1)
            quantize_g(0, 0)
            copy_l(0)
            group_g(0, 1)
            quantize_l(0)
            quantize_g(0, 1)
            multiply_h(0)
            multiply_h(1)
            multiply_h(2)
            log_v_pair(1)
            group_r(0, 0)
            load_r(1, 1)
            for k in range(1, TILES // 2):
                load_pair(m_raw, m, k)
            copy_h("scalar", 0)
            multiply_h(3)
            log_v_pair(2)
            copy_h("scalar", 1)
            quantize_r(0, 0)
            group_r(0, 1)
            copy_h("scalar", 2)
            quantize_h(0)
            quantize_r(0, 1)
            log_v_pair(3)
            turn_l(1)
            copy_h("scalar", 3)
            group_g(1, 0)
            copy_l(1)
            quantize_h(1)
            quantize_g(1, 0)
            group_g(1, 1)
            quantize_l(1)
            quantize_g(1, 1)
            for k in range(TILES // 2):
                sigmoid_pair(k)
            multiply_h(4)
            multiply_h(5)
            group_r(1, 0)
            copy_h("vector", 4)
            quantize_r(1, 0)
            copy_h("vector", 5)
            times_m_pair(0)
            quantize_h(2)
            multiply_h(6)
            multiply_h(7)
            group_r(1, 1)
            copy_h("scalar", 6)
            times_m_pair(1)
            multiply_p(0)
            square_p(0)
            square_a(0)
            root_p(0)
            square_a(1)
            copy_h("scalar", 7)
            root_a(0)
            divisor(0)
            quantize_r(1, 1)
            inverse(0)
            quantize_h(3)
            factor(0)
            multiply_p(1)
            square_p(1)
            square_a(2)
            for t in range(TILES - 2):
                multiply_p(t + 2)
                if t >= 1:
                    copy_out(t - 1)
                root_p(t + 1)
                mix(t, 0)
                mix(t, 1)
                store_out(t)
                divisor(t + 1)
                round_out("vector", t, 0)
                inverse(t + 1)
                round_out("vector", t, 1)
                turn_out(t)
                if t + 3 < TILES:
                    square_a(t + 3)
                square_p(t + 2)
                if t % 2 == 0 and t + 3 < TILES:
                    root_a(t + 2)
                if t >= 1:
                    quantize_out(t - 1)
                    store_words(t - 1)
                factor(t + 1)
                if t == ROW_TILES:
                    store_scales(0)
                if t + 4 < TILES:
                    times_m(t + 4)
            a, b, c = TILES - 3, TILES - 2, TILES - 1
            root_p(c)
            copy_out(a)
            mix(b, 0)
            round_out("scalar", b, 0)
            mix(b, 1)
            store_out(b)
            round_out("scalar", b, 1)
            divisor(c)
            quantize_out(a)
            store_words(a)
            inverse(c)
            factor(c)
            turn_out(b)
            mix(c, 0)
            store_out_half(c, 0)
            mix(c, 1)
            store_out_half(c, 1)
            round_out("scalar", c, 0)
            copy_out(b)
            round_out("vector", c, 1)
            turn_out(c)
            quantize_out(b)
            store_words(b)
            copy_out_group("scalar", c, 0)
            copy_out_group("vector", c, 1)
            quantize_out(c)
            store_words(c)
            store_scales(1)
